import numpy as np
import ml_dtypes


def mxq(x, axis, fmt="e4m3"):
    dtype, down = {"e4m3": (ml_dtypes.float8_e4m3fn, 7), "e5m2": (ml_dtypes.float8_e5m2, 14)}[fmt]
    v = np.moveaxis(np.asarray(x, np.float32).astype(ml_dtypes.bfloat16).astype(np.float64), axis, -1)
    blocks = v.reshape(v.shape[:-1] + (-1, 32))
    amax = np.abs(blocks).max(-1, keepdims=True)
    byte = np.maximum(np.where(amax > 0, np.frexp(amax)[1] - 1 + 127, 0) - down, 1)
    scale = np.exp2(byte - 127.0)
    codes = (blocks / scale).astype(np.float32).astype(dtype).astype(np.float64)
    return np.moveaxis((codes * scale).reshape(v.shape), -1, axis)


WIDE = False


def mx_kscale(k):
    if not WIDE:
        return np.ones(k)
    levels = np.array([10, -10, 5, -5, 0])
    if k % 512:
        return np.exp2(np.random.permutation(np.resize(levels, k // 32))).repeat(32)
    a = np.empty((k // 512, 16))
    for p in range(k // 512):
        a[p, :8] = np.random.permutation(np.resize(levels, 8))
        for g in range(8):
            far = levels[np.abs(levels - a[p, g]) >= 10]
            a[p, g + 8] = far[np.random.randint(len(far))]
    return np.exp2(a.ravel()).repeat(32)


def f64(x):
    return np.asarray(x).astype(np.float64)


def striped(idx):
    return np.tile(idx.reshape(-1, 16).T, (8, 1)).astype(np.uint16)


def unstriped(offs):
    return offs[:16].T.reshape(-1).astype(np.int64)


def pack_weight(w):
    k, n = w.shape
    w = f64(np.asarray(w, np.float32).astype(ml_dtypes.bfloat16)).reshape(k // 32, 32, n)
    amax = np.abs(w).max(1)
    byte = np.clip(np.where(amax > 0, np.frexp(amax)[1] - 1 + 127 - 7, 1), 1, 254)
    scaled = (w * np.exp2(127.0 - byte)[:, None, :]).reshape(k, n).astype(np.float32)
    words = np.ascontiguousarray(scaled.reshape(k // 512, 128, 4, n).transpose(0, 1, 3, 2)).astype(ml_dtypes.float8_e4m3fn).view(np.uint8)
    return words, np.ascontiguousarray(byte.astype(np.uint8).reshape(k // 512, 16, n))


def unpack_weight(words, scales):
    g, p, n, _ = words.shape
    vals = np.ascontiguousarray(words).view(ml_dtypes.float8_e4m3fn).astype(np.float64) * np.repeat(np.exp2(scales.astype(np.float64) - 127.0), 8, axis=1)[..., None]
    return vals.transpose(0, 1, 3, 2).reshape(g * 512, n)


def planes(y):
    n, m = y.shape
    v = y.astype(np.float32).astype(ml_dtypes.bfloat16).astype(np.float64).reshape(n // 32, 32, m)
    top = np.abs(v).max(1)
    byte = np.clip(np.where(top > 0, np.frexp(top)[1] - 1 + 127 - 7, 1), 1, 254)
    codes = (v * np.exp2(127.0 - byte)[:, None, :]).reshape(n, m).astype(np.float32).astype(ml_dtypes.float8_e4m3fn).view(np.uint8)
    words = codes.reshape(n // 512, 128, 4, m).transpose(0, 1, 3, 2)
    return np.ascontiguousarray(words), np.ascontiguousarray(byte.astype(np.uint8).reshape(n // 512, 16, m))


def relu(v):
    return np.maximum(v, 0.0)


K, T, S, N = 512, 4096, 1024, 512


def setup_inputs():
    n = np.random.standard_normal
    s = mx_kscale(K)[:, None]
    packed_xT = pack_weight(n((K, T)) * s)
    return {
        "x_words": packed_xT[0],
        "x_scales": packed_xT[1],
        "w1": (n((K, N)) / np.sqrt(K) / s).astype(np.float32),
        "dual": (np.random.uniform(-1.0, 1.0, (N, S))).astype(np.float32),
        "data": (n((N, S))).astype(np.float32),
        "offs": striped(np.random.permutation(T)[:S]),
    }


def reference(x_words, x_scales, w1, dual, data, offs):
    xq = unpack_weight(x_words, x_scales)[:, unstriped(offs)]
    y = mxq(f64(w1), 0, "e4m3").T @ xq
    p1 = f64(dual) + 0.4 * (np.pad(y, ((0, 0), (0, 1)))[:, 1:] - y)
    pc = p1 - relu(p1 - 1.0) + relu(-1.0 * p1 - 1.0)
    div = pc - (np.pad(pc, ((0, 0), (1, 0)))[:, :S])
    un = (y + 0.4 * div + 0.8 * f64(data)) / 1.8
    out_0 = 2.0 * un - y
    return (out_0,) + planes(out_0)

@@ -1,0 +1,190 @@
+from contextlib import ExitStack
+
+import concourse.mybir as mybir
+
+K, T, S, N = 512, 4096, 1024, 512
+FLOPS = 2 * K * N * S
+BYTES = K * T + (K // 32) * T + 4 * K * N + 3 * 4 * N * S + N * S + (N // 32) * S + 2 * 128 * (S // 16)
+
+F32 = mybir.dt.float32
+BF16 = mybir.dt.bfloat16
+I32 = mybir.dt.int32
+U32 = mybir.dt.uint32
+U16 = mybir.dt.uint16
+U8 = mybir.dt.uint8
+FP8X4 = mybir.dt.float8_e4m3fn_x4
+ALU = mybir.AluOpType
+RELU = mybir.ActivationFunctionType.Relu
+
+P = 128
+PACK = 4
+CH = 128
+NCH = S // CH
+LD = 256
+PAD = 8
+G_CHUNKS = 6
+
+
+def tile_picked_ytvpd_bar_po_kernel(
+    tc, x_words, x_scales, w1, dual, data, offs, out_0, out_1, out_2
+):
+    nc = tc.nc
+    with ExitStack() as ctx:
+        keep = ctx.enter_context(tc.tile_pool(name="keep", bufs=1))
+        head = ctx.enter_context(tc.tile_pool(name="head", bufs=1))
+        ring = ctx.enter_context(tc.tile_pool(name="ring", bufs=3))
+        psum = ctx.enter_context(tc.psum_pool(name="psum", bufs=1))
+
+        offsets = keep.tile([P, S // 16], U16, name="offsets")
+        nc.sync.dma_start(offsets[:], offs)
+
+        x_table = keep.tile([P, T], I32, name="x_table", align_bytes=64)
+        nc.sync.dma_start(x_table[:], x_words[0].rearrange("p c r -> p (c r)").bitcast(I32))
+
+        s_table = head.tile([P, T], U8, name="s_table", offset=2048, align_bytes=64)
+        nc.vector.memset(s_table[:].bitcast(I32), 0)
+        s_rows = x_scales[0].bitcast(I32).rearrange("(q r) c -> r q c", r=4)
+        for r in range(4):
+            nc.scalar.dma_start(s_table[:].bitcast(I32)[r:P:32, :], s_rows[r])
+
+        w_view = w1.rearrange("(p j) c -> p j c", j=PACK)
+        w_raw = []
+        for h in range(2):
+            w_half = keep.tile([P, PACK, N // 2], F32, name="w_raw%d" % h)
+            nc.sync.dma_start(w_half[:], w_view[:, :, h * 256 : (h + 1) * 256])
+            w_raw.append(w_half)
+
+        x_bytes = keep.tile([P, S], U8, name="x_bytes", align_bytes=64)
+        nc.vector.tensor_copy(x_bytes[:], s_table[:].indirect(offsets[:]))
+        x_codes = head.tile([P, S], U32, name="x_codes", offset=0, align_bytes=64)
+        nc.vector.tensor_copy(x_codes[:], x_table[:].bitcast(U32).indirect(offsets[:]))
+
+        dual_view = dual.rearrange("(p t) j -> p t j", t=PACK)
+        data_view = data.rearrange("(p t) j -> p t j", t=PACK)
+        out_view = out_0.rearrange("(p t) j -> p t j", t=PACK)
+        work = head.tile([P, 2, PACK, PAD + S], F32, name="work", offset=4096, align_bytes=64)
+        acc = work[:, 0]
+        base = work[:, 1]
+        nc.gpsimd.memset(acc[:, :, 0:PAD], 0.0)
+        lines = [keep.tile([P, PACK, LD], F32, name="lines%d" % b) for b in range(S // LD)]
+        for b in range(S // LD):
+            nc.sync.dma_start(acc[:, :, PAD + b * LD : PAD + (b + 1) * LD], dual_view[:, :, b * LD : (b + 1) * LD])
+            nc.sync.dma_start(base[:, :, b * LD : (b + 1) * LD], data_view[:, :, b * LD : (b + 1) * LD])
+
+        one = keep.tile([P, 1], F32, name="one")
+        nc.gpsimd.memset(one[:], 1.0)
+        two_c = keep.tile([P, 1], F32, name="two_c")
+        nc.scalar.activation(two_c[:], one[:], RELU, scale=8.0 / 9.0)
+
+        w_grouped = keep.tile([P, PACK, P, PACK], BF16, name="w_grouped", align_bytes=64)
+        nc.scalar.copy(
+            w_grouped[:, :, 0:64, :].rearrange("p t m j -> p m j t"),
+            w_raw[0][:].rearrange("p j (m t) -> p m j t", t=PACK),
+        )
+        nc.vector.tensor_copy(
+            w_grouped[:, :, 64:128, :].rearrange("p t m j -> p m j t"),
+            w_raw[1][:].rearrange("p j (m t) -> p m j t", t=PACK),
+        )
+        w_codes = keep.tile([P, N], U32, name="w_codes", align_bytes=64)
+        w_bytes = keep.tile([P, N], U8, name="w_bytes", align_bytes=64)
+        nc.vector.quantize_mx(
+            out=w_codes[:].bitcast(FP8X4),
+            scales=w_bytes[:],
+            in_=w_grouped[:].rearrange("p t m j -> p (t m j)"),
+        )
+
+        y = [psum.tile([P, PACK, CH], F32, name="y%d" % c) for c in range(NCH)]
+        for c in range(NCH):
+            for t in range(PACK):
+                nc.tensor.matmul_mx(
+                    out=y[c][:, t, :],
+                    lhsT=w_codes[:, t * P : (t + 1) * P].bitcast(FP8X4),
+                    lhsT_scale=w_bytes[:, t * P : (t + 1) * P],
+                    rhs=x_codes[:, c * CH : (c + 1) * CH].bitcast(FP8X4),
+                    rhs_scale=x_bytes[:, c * CH : (c + 1) * CH],
+                    start=True,
+                    stop=True,
+                )
+
+        o_codes = keep.tile([P, S], U32, name="o_codes", align_bytes=64)
+        o_bytes = keep.tile([P, S], U8, name="o_bytes", align_bytes=64)
+        words_view = out_1[0].rearrange("p c r -> p (c r)").bitcast(I32)
+        slack = {}
+        diff = {}
+        rounded = {}
+
+        def line_cols(c):
+            off = (c * CH) % LD
+            return lines[(c * CH) // LD][:, :, off : off + CH]
+
+        def add_next(c):
+            first = 1 if c == 0 else 0
+            cols = acc[:, :, PAD + c * CH - 1 + first : PAD + (c + 1) * CH - 1]
+            nc.vector.scalar_tensor_tensor(cols, y[c][:, :, first:CH], 0.4, cols, ALU.mult, ALU.add)
+
+        def sub_here(c):
+            cols = acc[:, :, PAD + c * CH : PAD + (c + 1) * CH]
+            nc.vector.scalar_tensor_tensor(cols, y[c][:], -0.4, cols, ALU.mult, ALU.add)
+
+        def clip(c):
+            cols = acc[:, :, PAD + c * CH - 1 : PAD + (c + 1) * CH]
+            raised = ring.tile([P, PACK, CH + 1], F32, name="raised")
+            nc.scalar.activation(raised[:], cols, RELU, bias=one[:], scale=1.0)
+            slack[c] = ring.tile([P, PACK * (CH + 1)], F32, name="slack")
+            nc.scalar.activation(slack[c][:], raised[:].rearrange("p t j -> p (t j)"), RELU, bias=two_c[:], scale=-4.0 / 9.0)
+
+        def divergence(c):
+            n = PACK * (CH + 1) - 1
+            diff[c] = keep.tile([P, PACK * (CH + 1)], F32, name="diff")
+            engine = nc.gpsimd if c < G_CHUNKS else nc.vector
+            engine.tensor_tensor(diff[c][:, 0:n], slack[c][:, 0:n], slack[c][:, 1 : n + 1], ALU.subtract)
+
+        def add_data(c):
+            cols = line_cols(c)
+            d = diff[c][:].rearrange("p (t j) -> p t j", t=PACK)[:, :, 0:CH]
+            nc.vector.scalar_tensor_tensor(cols, base[:, :, c * CH : (c + 1) * CH], 8.0 / 9.0, d, ALU.mult, ALU.add)
+
+        def add_primal(c):
+            cols = base[:, :, c * CH : (c + 1) * CH]
+            nc.vector.scalar_tensor_tensor(cols, y[c][:], 0.125, cols, ALU.mult, ALU.add)
+
+        def round_out(c):
+            rounded[c] = ring.tile([P, CH, PACK], BF16, name="rounded", align_bytes=64)
+            nc.scalar.copy(
+                rounded[c][:].rearrange("p (g i) t -> p g t i", i=4),
+                line_cols(c).rearrange("p t (g i) -> p g t i", i=4),
+            )
+            if (c + 1) * CH % LD == 0:
+                b = (c * CH) // LD
+                nc.sync.dma_start(out_view[:, :, b * LD : (b + 1) * LD], lines[b][:])
+
+        def quantise(c):
+            nc.vector.quantize_mx(
+                out=o_codes[:, c * CH : (c + 1) * CH].bitcast(FP8X4),
+                scales=o_bytes[:, c * CH : (c + 1) * CH],
+                in_=rounded[c][:].rearrange("p j t -> p (j t)"),
+            )
+            if (c + 1) * CH % 512 == 0:
+                lo = (c + 1) * CH - 512
+                nc.sync.dma_start(words_view[:, lo : lo + 512], o_codes[:, lo : lo + 512].bitcast(I32))
+
+        stages = [
+            (quantise, 6),
+            (add_data, 4),
+            (divergence, 3),
+            (sub_here, 0),
+            (add_next, -2),
+            (clip, 1),
+            (add_primal, 2),
+            (round_out, 4),
+        ]
+        for step in range(-2, NCH + 6):
+            for stage, lag in stages:
+                c = step - lag
+                if 0 <= c < NCH:
+                    stage(c)
+
+        scale_rows = out_2[0].bitcast(I32).rearrange("(q r) c -> q r c", r=4)
+        for q in range(4):
+            queue = nc.sync if q % 2 == 0 else nc.scalar
+            queue.dma_start(scale_rows[q], o_bytes[:].bitcast(I32)[32 * q : 32 * q + 4, :])

@@ -22,7 +22,10 @@ CH = 128
 NCH = S // CH
 LD = 256
 PAD = 8
-G_CHUNKS = 6
+QUANT = [(0, 512), (512, 768), (768, 896), (896, 1024)]
+WORDS = [(0, 896), (896, 1024)]
+G_CHUNKS = 7
+X_FIRST = [256,256,256,256,256]
 
 
 def tile_picked_ytvpd_bar_po_kernel(
@@ -32,6 +35,7 @@ def tile_picked_ytvpd_bar_po_kernel(
     with ExitStack() as ctx:
         keep = ctx.enter_context(tc.tile_pool(name="keep", bufs=1))
         head = ctx.enter_context(tc.tile_pool(name="head", bufs=1))
+        late = ctx.enter_context(tc.tile_pool(name="late", bufs=1))
         ring = ctx.enter_context(tc.tile_pool(name="ring", bufs=3))
         psum = ctx.enter_context(tc.psum_pool(name="psum", bufs=1))
 
@@ -39,13 +43,16 @@ def tile_picked_ytvpd_bar_po_kernel(
         nc.sync.dma_start(offsets[:], offs)
 
         x_table = keep.tile([P, T], I32, name="x_table", align_bytes=64)
-        nc.sync.dma_start(x_table[:], x_words[0].rearrange("p c r -> p (c r)").bitcast(I32))
+        x_view = x_words[0].rearrange("p c r -> p (c r)").bitcast(I32)
+        lo = 0
+        for width in X_FIRST:
+            nc.sync.dma_start(x_table[:, lo : lo + width], x_view[:, lo : lo + width])
+            lo = lo + width
 
-        s_table = head.tile([P, T], U8, name="s_table", offset=2048, align_bytes=64)
+        s_table = head.tile([P, T], U8, name="s_table", offset=0, align_bytes=64)
         nc.vector.memset(s_table[:].bitcast(I32), 0)
-        s_rows = x_scales[0].bitcast(I32).rearrange("(q r) c -> r q c", r=4)
-        for r in range(4):
-            nc.scalar.dma_start(s_table[:].bitcast(I32)[r:P:32, :], s_rows[r])
+        nc.sync.dma_start(s_table[:].bitcast(I32)[0:P:8, :], x_scales[0].bitcast(I32))
+        nc.sync.dma_start(x_table[:, lo:T], x_view[:, lo:T])
 
         w_view = w1.rearrange("(p j) c -> p j c", j=PACK)
         w_raw = []
@@ -54,15 +61,19 @@ def tile_picked_ytvpd_bar_po_kernel(
             nc.sync.dma_start(w_half[:], w_view[:, :, h * 256 : (h + 1) * 256])
             w_raw.append(w_half)
 
+        picked = keep.tile([P, S], U8, name="picked", align_bytes=64)
+        nc.vector.tensor_copy(picked[:], s_table[:].indirect(offsets[:]))
         x_bytes = keep.tile([P, S], U8, name="x_bytes", align_bytes=64)
-        nc.vector.tensor_copy(x_bytes[:], s_table[:].indirect(offsets[:]))
-        x_codes = head.tile([P, S], U32, name="x_codes", offset=0, align_bytes=64)
+        nc.vector.memset(x_bytes[:].bitcast(I32), 0)
+        for r in range(4):
+            nc.sync.dma_start(x_bytes[:].bitcast(I32)[r:P:32, :], picked[:].bitcast(I32)[8 * r : P : 32, :])
+        x_codes = keep.tile([P, S], U32, name="x_codes", align_bytes=64)
         nc.vector.tensor_copy(x_codes[:], x_table[:].bitcast(U32).indirect(offsets[:]))
 
         dual_view = dual.rearrange("(p t) j -> p t j", t=PACK)
         data_view = data.rearrange("(p t) j -> p t j", t=PACK)
         out_view = out_0.rearrange("(p t) j -> p t j", t=PACK)
-        work = head.tile([P, 2, PACK, PAD + S], F32, name="work", offset=4096, align_bytes=64)
+        work = head.tile([P, 2, PACK, PAD + S], F32, name="work", offset=0, align_bytes=64)
         acc = work[:, 0]
         base = work[:, 1]
         nc.gpsimd.memset(acc[:, :, 0:PAD], 0.0)
@@ -81,17 +92,17 @@ def tile_picked_ytvpd_bar_po_kernel(
             w_grouped[:, :, 0:64, :].rearrange("p t m j -> p m j t"),
             w_raw[0][:].rearrange("p j (m t) -> p m j t", t=PACK),
         )
-        nc.vector.tensor_copy(
-            w_grouped[:, :, 64:128, :].rearrange("p t m j -> p m j t"),
-            w_raw[1][:].rearrange("p j (m t) -> p m j t", t=PACK),
-        )
+        w_last = w_raw[1][:].rearrange("p j (m t) -> p m j t", t=PACK)
+        nc.vector.tensor_copy(w_grouped[:, :, 64:104, :].rearrange("p t m j -> p m j t"), w_last[:, 0:40])
+        nc.scalar.copy(w_grouped[:, :, 104:128, :].rearrange("p t m j -> p m j t"), w_last[:, 40:64])
         w_codes = keep.tile([P, N], U32, name="w_codes", align_bytes=64)
         w_bytes = keep.tile([P, N], U8, name="w_bytes", align_bytes=64)
-        nc.vector.quantize_mx(
-            out=w_codes[:].bitcast(FP8X4),
-            scales=w_bytes[:],
-            in_=w_grouped[:].rearrange("p t m j -> p (t m j)"),
-        )
+        for h in range(2):
+            nc.vector.quantize_mx(
+                out=w_codes[:, h * 256 : (h + 1) * 256].bitcast(FP8X4),
+                scales=w_bytes[:, h * 256 : (h + 1) * 256],
+                in_=w_grouped[:, 2 * h : 2 * h + 2].rearrange("p t m j -> p (t m j)"),
+            )
 
         y = [psum.tile([P, PACK, CH], F32, name="y%d" % c) for c in range(NCH)]
         for c in range(NCH):
@@ -106,12 +117,11 @@ def tile_picked_ytvpd_bar_po_kernel(
                     stop=True,
                 )
 
-        o_codes = keep.tile([P, S], U32, name="o_codes", align_bytes=64)
         o_bytes = keep.tile([P, S], U8, name="o_bytes", align_bytes=64)
         words_view = out_1[0].rearrange("p c r -> p (c r)").bitcast(I32)
+        rounded = keep.tile([P, S, PACK], BF16, name="rounded", align_bytes=64)
         slack = {}
         diff = {}
-        rounded = {}
 
         def line_cols(c):
             off = (c * CH) % LD
@@ -135,8 +145,12 @@ def tile_picked_ytvpd_bar_po_kernel(
 
         def divergence(c):
             n = PACK * (CH + 1) - 1
-            diff[c] = keep.tile([P, PACK * (CH + 1)], F32, name="diff")
-            engine = nc.gpsimd if c < G_CHUNKS else nc.vector
+            if c < G_CHUNKS:
+                diff[c] = late.tile([P, PACK * (CH + 1)], F32, name="diff_pool", offset=0, align_bytes=64)
+                engine = nc.gpsimd
+            else:
+                diff[c] = ring.tile([P, PACK * (CH + 1)], F32, name="diff_vector")
+                engine = nc.vector
             engine.tensor_tensor(diff[c][:, 0:n], slack[c][:, 0:n], slack[c][:, 1 : n + 1], ALU.subtract)
 
         def add_data(c):
@@ -149,27 +163,20 @@ def tile_picked_ytvpd_bar_po_kernel(
             nc.vector.scalar_tensor_tensor(cols, y[c][:], 0.125, cols, ALU.mult, ALU.add)
 
         def round_out(c):
-            rounded[c] = ring.tile([P, CH, PACK], BF16, name="rounded", align_bytes=64)
-            nc.scalar.copy(
-                rounded[c][:].rearrange("p (g i) t -> p g t i", i=4),
-                line_cols(c).rearrange("p t (g i) -> p g t i", i=4),
-            )
-            if (c + 1) * CH % LD == 0:
+            dst = rounded[:, c * CH : (c + 1) * CH, :].rearrange("p (g i) t -> p g t i", i=4)
+            src = line_cols(c).rearrange("p t (g i) -> p g t i", i=4)
+            if c < NCH - 1:
+                nc.scalar.copy(dst, src)
+            else:
+                nc.scalar.copy(dst[:, 0:12], src[:, 0:12])
+                nc.vector.tensor_copy(dst[:, 12:32], src[:, 12:32])
+            if c >= NCH - 2:
+                nc.sync.dma_start(out_view[:, :, c * CH : (c + 1) * CH], line_cols(c))
+            elif (c + 1) * CH % LD == 0:
                 b = (c * CH) // LD
                 nc.sync.dma_start(out_view[:, :, b * LD : (b + 1) * LD], lines[b][:])
 
-        def quantise(c):
-            nc.vector.quantize_mx(
-                out=o_codes[:, c * CH : (c + 1) * CH].bitcast(FP8X4),
-                scales=o_bytes[:, c * CH : (c + 1) * CH],
-                in_=rounded[c][:].rearrange("p j t -> p (j t)"),
-            )
-            if (c + 1) * CH % 512 == 0:
-                lo = (c + 1) * CH - 512
-                nc.sync.dma_start(words_view[:, lo : lo + 512], o_codes[:, lo : lo + 512].bitcast(I32))
-
         stages = [
-            (quantise, 6),
             (add_data, 4),
             (divergence, 3),
             (sub_here, 0),
@@ -178,11 +185,21 @@ def tile_picked_ytvpd_bar_po_kernel(
             (add_primal, 2),
             (round_out, 4),
         ]
-        for step in range(-2, NCH + 6):
+        for step in range(-2, NCH + 4):
             for stage, lag in stages:
                 c = step - lag
                 if 0 <= c < NCH:
                     stage(c)
+
+        o_codes = late.tile([P, S], U32, name="o_codes", offset=0, align_bytes=64)
+        for lo, hi in QUANT:
+            nc.vector.quantize_mx(
+                out=o_codes[:, lo:hi].bitcast(FP8X4),
+                scales=o_bytes[:, lo:hi],
+                in_=rounded[:, lo:hi, :].rearrange("p j t -> p (j t)"),
+            )
+        for lo, hi in WORDS:
+            nc.sync.dma_start(words_view[:, lo:hi], o_codes[:, lo:hi].bitcast(I32))
 
         scale_rows = out_2[0].bitcast(I32).rearrange("(q r) c -> q r c", r=4)
         for q in range(4):

@@ -4,7 +4,6 @@ import concourse.mybir as mybir
 
 K, T, S, N = 512, 4096, 1024, 512
 FLOPS = 2 * K * N * S
-BYTES = K * T + (K // 32) * T + 4 * K * N + 3 * 4 * N * S + N * S + (N // 32) * S + 2 * 128 * (S // 16)
 
 F32 = mybir.dt.float32
 BF16 = mybir.dt.bfloat16
@@ -14,18 +13,22 @@ U16 = mybir.dt.uint16
 U8 = mybir.dt.uint8
 FP8X4 = mybir.dt.float8_e4m3fn_x4
 ALU = mybir.AluOpType
+COPY = mybir.ActivationFunctionType.Copy
 RELU = mybir.ActivationFunctionType.Relu
 
 P = 128
 PACK = 4
-CH = 128
-NCH = S // CH
-LD = 256
+CHUNK = 128
+CHUNKS = S // CHUNK
+HALF = S // 2
 PAD = 8
+ZERO_SPLIT = 704
+POOL_CHUNKS = 3
+DUAL_STEPS_FIRST = 11
+POOL_SPANS = [(0, CHUNK), (CHUNK, 3 * CHUNK), (3 * CHUNK, 5 * CHUNK)]
+LAST_SPAN = (5 * CHUNK, S)
+LAST_PIECES = [(640, 832), (832, 960), (960, 1024)]
 QUANT = [(0, 512), (512, 768), (768, 896), (896, 1024)]
-WORDS = [(0, 896), (896, 1024)]
-G_CHUNKS = 7
-X_FIRST = [256,256,256,256,256]
 
 
 def tile_picked_ytvpd_bar_po_kernel(
@@ -34,53 +37,36 @@ def tile_picked_ytvpd_bar_po_kernel(
     nc = tc.nc
     with ExitStack() as ctx:
         keep = ctx.enter_context(tc.tile_pool(name="keep", bufs=1))
-        head = ctx.enter_context(tc.tile_pool(name="head", bufs=1))
-        late = ctx.enter_context(tc.tile_pool(name="late", bufs=1))
-        ring = ctx.enter_context(tc.tile_pool(name="ring", bufs=3))
+        reused = ctx.enter_context(tc.tile_pool(name="reused", bufs=1))
         psum = ctx.enter_context(tc.psum_pool(name="psum", bufs=1))
 
         offsets = keep.tile([P, S // 16], U16, name="offsets")
         nc.sync.dma_start(offsets[:], offs)
 
-        x_table = keep.tile([P, T], I32, name="x_table", align_bytes=64)
-        x_view = x_words[0].rearrange("p c r -> p (c r)").bitcast(I32)
-        lo = 0
-        for width in X_FIRST:
-            nc.sync.dma_start(x_table[:, lo : lo + width], x_view[:, lo : lo + width])
-            lo = lo + width
-
-        s_table = head.tile([P, T], U8, name="s_table", offset=0, align_bytes=64)
-        nc.vector.memset(s_table[:].bitcast(I32), 0)
-        nc.sync.dma_start(s_table[:].bitcast(I32)[0:P:8, :], x_scales[0].bitcast(I32))
-        nc.sync.dma_start(x_table[:, lo:T], x_view[:, lo:T])
-
         w_view = w1.rearrange("(p j) c -> p j c", j=PACK)
-        w_raw = []
-        for h in range(2):
-            w_half = keep.tile([P, PACK, N // 2], F32, name="w_raw%d" % h)
-            nc.sync.dma_start(w_half[:], w_view[:, :, h * 256 : (h + 1) * 256])
-            w_raw.append(w_half)
+        w_raw = reused.tile([P, PACK, N], F32, name="w_raw", offset=0, align_bytes=64)
+        for j in range(PACK - 1):
+            nc.sync.dma_start(w_raw[:, j, :], w_view[:, j, :])
 
-        picked = keep.tile([P, S], U8, name="picked", align_bytes=64)
-        nc.vector.tensor_copy(picked[:], s_table[:].indirect(offsets[:]))
-        x_bytes = keep.tile([P, S], U8, name="x_bytes", align_bytes=64)
-        nc.vector.memset(x_bytes[:].bitcast(I32), 0)
+        scale_table = keep.tile([P, T], U8, name="scale_table", align_bytes=64)
+        nc.vector.memset(scale_table[:].bitcast(I32)[:, 0:ZERO_SPLIT], 0)
+        nc.gpsimd.memset(scale_table[:].bitcast(I32)[:, ZERO_SPLIT:], 0)
+        nc.sync.dma_start(scale_table[:].bitcast(I32)[0:P:8, :], x_scales[0].bitcast(I32))
+        nc.sync.dma_start(w_raw[:, PACK - 1, :], w_view[:, PACK - 1, :])
+
+        word_table = keep.tile([P, T], I32, name="word_table", align_bytes=64)
+        nc.sync.dma_start(word_table[:], x_words[0].rearrange("p c r -> p (c r)").bitcast(I32))
+
+        picked_scales = keep.tile([P, S], U8, name="picked_scales", align_bytes=64)
+        nc.vector.tensor_copy(picked_scales[:], scale_table[:].indirect(offsets[:]))
+        x_scale = keep.tile([P, S], U8, name="x_scale", align_bytes=64)
+        nc.vector.memset(x_scale[:].bitcast(I32), 0)
         for r in range(4):
-            nc.sync.dma_start(x_bytes[:].bitcast(I32)[r:P:32, :], picked[:].bitcast(I32)[8 * r : P : 32, :])
-        x_codes = keep.tile([P, S], U32, name="x_codes", align_bytes=64)
-        nc.vector.tensor_copy(x_codes[:], x_table[:].bitcast(U32).indirect(offsets[:]))
-
-        dual_view = dual.rearrange("(p t) j -> p t j", t=PACK)
-        data_view = data.rearrange("(p t) j -> p t j", t=PACK)
-        out_view = out_0.rearrange("(p t) j -> p t j", t=PACK)
-        work = head.tile([P, 2, PACK, PAD + S], F32, name="work", offset=0, align_bytes=64)
-        acc = work[:, 0]
-        base = work[:, 1]
-        nc.gpsimd.memset(acc[:, :, 0:PAD], 0.0)
-        lines = [keep.tile([P, PACK, LD], F32, name="lines%d" % b) for b in range(S // LD)]
-        for b in range(S // LD):
-            nc.sync.dma_start(acc[:, :, PAD + b * LD : PAD + (b + 1) * LD], dual_view[:, :, b * LD : (b + 1) * LD])
-            nc.sync.dma_start(base[:, :, b * LD : (b + 1) * LD], data_view[:, :, b * LD : (b + 1) * LD])
+            nc.sync.dma_start(x_scale[:].bitcast(I32)[r:P:32, :], picked_scales[:].bitcast(I32)[8 * r : P : 32, :])
+        x_codes = [keep.tile([P, HALF], U32, name="x_codes%d" % h, align_bytes=64) for h in range(2)]
+        for h in range(2):
+            entries = offsets[:, h * HALF // 16 : (h + 1) * HALF // 16]
+            nc.vector.tensor_copy(x_codes[h][:], word_table[:].bitcast(U32).indirect(entries))
 
         one = keep.tile([P, 1], F32, name="one")
         nc.gpsimd.memset(one[:], 1.0)
@@ -89,119 +75,153 @@ def tile_picked_ytvpd_bar_po_kernel(
 
         w_grouped = keep.tile([P, PACK, P, PACK], BF16, name="w_grouped", align_bytes=64)
         nc.scalar.copy(
-            w_grouped[:, :, 0:64, :].rearrange("p t m j -> p m j t"),
-            w_raw[0][:].rearrange("p j (m t) -> p m j t", t=PACK),
+            w_grouped[:].rearrange("p t m j -> p m j t"),
+            w_raw[:].rearrange("p j (m t) -> p m j t", t=PACK),
         )
-        w_last = w_raw[1][:].rearrange("p j (m t) -> p m j t", t=PACK)
-        nc.vector.tensor_copy(w_grouped[:, :, 64:104, :].rearrange("p t m j -> p m j t"), w_last[:, 0:40])
-        nc.scalar.copy(w_grouped[:, :, 104:128, :].rearrange("p t m j -> p m j t"), w_last[:, 40:64])
         w_codes = keep.tile([P, N], U32, name="w_codes", align_bytes=64)
-        w_bytes = keep.tile([P, N], U8, name="w_bytes", align_bytes=64)
-        for h in range(2):
-            nc.vector.quantize_mx(
-                out=w_codes[:, h * 256 : (h + 1) * 256].bitcast(FP8X4),
-                scales=w_bytes[:, h * 256 : (h + 1) * 256],
-                in_=w_grouped[:, 2 * h : 2 * h + 2].rearrange("p t m j -> p (t m j)"),
-            )
+        w_scale = keep.tile([P, N], U8, name="w_scale", align_bytes=64)
+        nc.vector.quantize_mx(
+            out=w_codes[:].bitcast(FP8X4),
+            scales=w_scale[:],
+            in_=w_grouped[:].rearrange("p t m j -> p (t m j)"),
+        )
 
-        y = [psum.tile([P, PACK, CH], F32, name="y%d" % c) for c in range(NCH)]
-        for c in range(NCH):
+        dual_view = dual.rearrange("(p t) j -> p t j", t=PACK)
+        data_view = data.rearrange("(p t) j -> p t j", t=PACK)
+        out_view = out_0.rearrange("(p t) j -> p t j", t=PACK)
+        lines = reused.tile([P, 2, PACK, PAD + S], F32, name="lines", offset=0, align_bytes=64)
+        moved = lines[:, 0]
+        primal = lines[:, 1]
+        nc.gpsimd.memset(moved[:, :, 0:PAD], 0.0)
+
+        def load_dual(lo, hi):
+            nc.sync.dma_start(moved[:, :, PAD + lo : PAD + hi], dual_view[:, :, lo:hi])
+
+        def load_data(lo, hi):
+            nc.sync.dma_start(primal[:, :, lo:hi], data_view[:, :, lo:hi])
+
+        load_dual(0, 2 * CHUNK)
+        load_data(0, POOL_CHUNKS * CHUNK)
+        for lo in range(2 * CHUNK, S, 2 * CHUNK):
+            load_dual(lo, lo + 2 * CHUNK)
+        load_data(POOL_CHUNKS * CHUNK, S)
+
+        y = [psum.tile([P, PACK, CHUNK], F32, name="y%d" % c) for c in range(CHUNKS)]
+        for c in range(CHUNKS):
+            h, lo = divmod(c * CHUNK, HALF)
             for t in range(PACK):
                 nc.tensor.matmul_mx(
                     out=y[c][:, t, :],
                     lhsT=w_codes[:, t * P : (t + 1) * P].bitcast(FP8X4),
-                    lhsT_scale=w_bytes[:, t * P : (t + 1) * P],
-                    rhs=x_codes[:, c * CH : (c + 1) * CH].bitcast(FP8X4),
-                    rhs_scale=x_bytes[:, c * CH : (c + 1) * CH],
+                    lhsT_scale=w_scale[:, t * P : (t + 1) * P],
+                    rhs=x_codes[h][:, lo : lo + CHUNK].bitcast(FP8X4),
+                    rhs_scale=x_scale[:, c * CHUNK : (c + 1) * CHUNK],
                     start=True,
                     stop=True,
                 )
 
-        o_bytes = keep.tile([P, S], U8, name="o_bytes", align_bytes=64)
-        words_view = out_1[0].rearrange("p c r -> p (c r)").bitcast(I32)
-        rounded = keep.tile([P, S, PACK], BF16, name="rounded", align_bytes=64)
-        slack = {}
-        diff = {}
+        eighth = keep.tile([P, PACK, POOL_CHUNKS * CHUNK], F32, name="eighth")
+        for c in range(POOL_CHUNKS):
+            nc.scalar.activation(eighth[:, :, c * CHUNK : (c + 1) * CHUNK], y[c][:], COPY, scale=0.125)
+        early = primal[:, :, 0 : POOL_CHUNKS * CHUNK]
+        nc.gpsimd.tensor_tensor(early, early, eighth[:], ALU.add)
 
-        def line_cols(c):
-            off = (c * CH) % LD
-            return lines[(c * CH) // LD][:, :, off : off + CH]
+        rounded = keep.tile([P, S, PACK], BF16, name="rounded", align_bytes=64)
 
         def add_next(c):
             first = 1 if c == 0 else 0
-            cols = acc[:, :, PAD + c * CH - 1 + first : PAD + (c + 1) * CH - 1]
-            nc.vector.scalar_tensor_tensor(cols, y[c][:, :, first:CH], 0.4, cols, ALU.mult, ALU.add)
+            cols = moved[:, :, PAD + c * CHUNK - 1 + first : PAD + (c + 1) * CHUNK - 1]
+            nc.vector.scalar_tensor_tensor(cols, y[c][:, :, first:CHUNK], 0.4, cols, ALU.mult, ALU.add)
 
-        def sub_here(c):
-            cols = acc[:, :, PAD + c * CH : PAD + (c + 1) * CH]
+        def subtract_own(c):
+            cols = moved[:, :, PAD + c * CHUNK : PAD + (c + 1) * CHUNK]
             nc.vector.scalar_tensor_tensor(cols, y[c][:], -0.4, cols, ALU.mult, ALU.add)
 
-        def clip(c):
-            cols = acc[:, :, PAD + c * CH - 1 : PAD + (c + 1) * CH]
-            raised = ring.tile([P, PACK, CH + 1], F32, name="raised")
-            nc.scalar.activation(raised[:], cols, RELU, bias=one[:], scale=1.0)
-            slack[c] = ring.tile([P, PACK * (CH + 1)], F32, name="slack")
-            nc.scalar.activation(slack[c][:], raised[:].rearrange("p t j -> p (t j)"), RELU, bias=two_c[:], scale=-4.0 / 9.0)
-
-        def divergence(c):
-            n = PACK * (CH + 1) - 1
-            if c < G_CHUNKS:
-                diff[c] = late.tile([P, PACK * (CH + 1)], F32, name="diff_pool", offset=0, align_bytes=64)
-                engine = nc.gpsimd
-            else:
-                diff[c] = ring.tile([P, PACK * (CH + 1)], F32, name="diff_vector")
-                engine = nc.vector
-            engine.tensor_tensor(diff[c][:, 0:n], slack[c][:, 0:n], slack[c][:, 1 : n + 1], ALU.subtract)
-
-        def add_data(c):
-            cols = line_cols(c)
-            d = diff[c][:].rearrange("p (t j) -> p t j", t=PACK)[:, :, 0:CH]
-            nc.vector.scalar_tensor_tensor(cols, base[:, :, c * CH : (c + 1) * CH], 8.0 / 9.0, d, ALU.mult, ALU.add)
-
-        def add_primal(c):
-            cols = base[:, :, c * CH : (c + 1) * CH]
+        def add_eighth(c):
+            cols = primal[:, :, c * CHUNK : (c + 1) * CHUNK]
             nc.vector.scalar_tensor_tensor(cols, y[c][:], 0.125, cols, ALU.mult, ALU.add)
 
-        def round_out(c):
-            dst = rounded[:, c * CH : (c + 1) * CH, :].rearrange("p (g i) t -> p g t i", i=4)
-            src = line_cols(c).rearrange("p t (g i) -> p g t i", i=4)
-            if c < NCH - 1:
-                nc.scalar.copy(dst, src)
+        def clip(span):
+            lo, hi = span
+            width = hi - lo + 1
+            raised = keep.tile([P, PACK, width], F32, name="raised%d" % lo)
+            nc.scalar.activation(raised[:], moved[:, :, PAD + lo - 1 : PAD + hi], RELU, bias=one[:], scale=1.0)
+            slack = keep.tile([P, PACK * width], F32, name="slack%d" % lo)
+            flat = raised[:].rearrange("p t j -> p (t j)")
+            nc.scalar.activation(slack[:], flat, RELU, bias=two_c[:], scale=-4.0 / 9.0)
+            return slack
+
+        def difference(engine, slack, name):
+            count = slack.shape[1]
+            diff = keep.tile([P, count], F32, name=name)
+            engine.tensor_tensor(diff[:, 0 : count - 1], slack[:, 0 : count - 1], slack[:, 1:count], ALU.subtract)
+            return diff[:].rearrange("p (t j) -> p t j", t=PACK)
+
+        def combine(lo, hi, diff_cols):
+            result = keep.tile([P, PACK, hi - lo], F32, name="result%d" % lo)
+            nc.vector.scalar_tensor_tensor(result[:], primal[:, :, lo:hi], 8.0 / 9.0, diff_cols, ALU.mult, ALU.add)
+            return result
+
+        def hand_on(lo, hi, result):
+            nc.scalar.copy(
+                rounded[:, lo:hi, :].rearrange("p (g i) t -> p g t i", i=4),
+                result[:].rearrange("p t (g i) -> p g t i", i=4),
+            )
+            nc.sync.dma_start(out_view[:, :, lo:hi], result[:])
+
+        dual_steps = [(add_next, 0), (add_next, 1), (subtract_own, 0)]
+        for c in range(2, CHUNKS, 2):
+            dual_steps.extend([(add_next, c), (add_next, c + 1), (subtract_own, c - 1), (subtract_own, c)])
+        dual_steps.append((subtract_own, CHUNKS - 1))
+        slacks = {}
+        diffs = {}
+
+        def run_dual_steps(steps):
+            for step, c in steps:
+                step(c)
+                for span in POOL_SPANS + [LAST_SPAN]:
+                    if step is subtract_own and span[1] == (c + 1) * CHUNK:
+                        slacks[span] = clip(span)
+                        if span == POOL_SPANS[0]:
+                            diffs[span] = difference(nc.gpsimd, slacks[span], "pool_diff")
+
+        def finish_pool_span(u):
+            lo, hi = POOL_SPANS[u]
+            result = combine(lo, hi, diffs[lo, hi][:, :, 0 : hi - lo])
+            if u + 1 < len(POOL_SPANS):
+                diffs[POOL_SPANS[u + 1]] = difference(nc.gpsimd, slacks[POOL_SPANS[u + 1]], "pool_diff")
             else:
-                nc.scalar.copy(dst[:, 0:12], src[:, 0:12])
-                nc.vector.tensor_copy(dst[:, 12:32], src[:, 12:32])
-            if c >= NCH - 2:
-                nc.sync.dma_start(out_view[:, :, c * CH : (c + 1) * CH], line_cols(c))
-            elif (c + 1) * CH % LD == 0:
-                b = (c * CH) // LD
-                nc.sync.dma_start(out_view[:, :, b * LD : (b + 1) * LD], lines[b][:])
+                diffs[LAST_SPAN] = difference(nc.vector, slacks[LAST_SPAN], "last_diff")
+            hand_on(lo, hi, result)
 
-        stages = [
-            (add_data, 4),
-            (divergence, 3),
-            (sub_here, 0),
-            (add_next, -2),
-            (clip, 1),
-            (add_primal, 2),
-            (round_out, 4),
-        ]
-        for step in range(-2, NCH + 4):
-            for stage, lag in stages:
-                c = step - lag
-                if 0 <= c < NCH:
-                    stage(c)
+        run_dual_steps(dual_steps[:DUAL_STEPS_FIRST])
+        finish_pool_span(0)
+        run_dual_steps(dual_steps[DUAL_STEPS_FIRST:])
+        finish_pool_span(1)
+        for c in range(POOL_CHUNKS, CHUNKS):
+            add_eighth(c)
+        finish_pool_span(2)
 
-        o_codes = late.tile([P, S], U32, name="o_codes", offset=0, align_bytes=64)
-        for lo, hi in QUANT:
+        out_codes = keep.tile([P, S], U32, name="out_codes", align_bytes=64)
+        out_scale = keep.tile([P, S], U8, name="out_scale", align_bytes=64)
+        words_view = out_1[0].rearrange("p c r -> p (c r)").bitcast(I32)
+
+        def quantise(lo, hi):
             nc.vector.quantize_mx(
-                out=o_codes[:, lo:hi].bitcast(FP8X4),
-                scales=o_bytes[:, lo:hi],
+                out=out_codes[:, lo:hi].bitcast(FP8X4),
+                scales=out_scale[:, lo:hi],
                 in_=rounded[:, lo:hi, :].rearrange("p j t -> p (j t)"),
             )
-        for lo, hi in WORDS:
-            nc.sync.dma_start(words_view[:, lo:hi], o_codes[:, lo:hi].bitcast(I32))
+            if hi % HALF == 0:
+                nc.sync.dma_start(words_view[:, hi - HALF : hi], out_codes[:, hi - HALF : hi].bitcast(I32))
+
+        quantise(*QUANT[0])
+        for lo, hi in LAST_PIECES:
+            hand_on(lo, hi, combine(lo, hi, diffs[LAST_SPAN][:, :, lo - LAST_SPAN[0] : hi - LAST_SPAN[0]]))
+        for lo, hi in QUANT[1:]:
+            quantise(lo, hi)
 
         scale_rows = out_2[0].bitcast(I32).rearrange("(q r) c -> q r c", r=4)
         for q in range(4):
             queue = nc.sync if q % 2 == 0 else nc.scalar
-            queue.dma_start(scale_rows[q], o_bytes[:].bitcast(I32)[32 * q : 32 * q + 4, :])
+            queue.dma_start(scale_rows[q], out_scale[:].bitcast(I32)[32 * q : 32 * q + 4, :])

@@ -27,8 +27,9 @@ POOL_CHUNKS = 3
 DUAL_STEPS_FIRST = 11
 POOL_SPANS = [(0, CHUNK), (CHUNK, 3 * CHUNK), (3 * CHUNK, 5 * CHUNK)]
 LAST_SPAN = (5 * CHUNK, S)
-LAST_PIECES = [(640, 832), (832, 960), (960, 1024)]
-QUANT = [(0, 512), (512, 768), (768, 896), (896, 1024)]
+LAST_PIECES = [(640, 832), (832, 1024)]
+VECTOR_ROUNDS = 96
+QUANT = [(0, 512), (512, 768), (768, 1024)]
 
 
 def tile_picked_ytvpd_bar_po_kernel(
@@ -162,11 +163,15 @@ def tile_picked_ytvpd_bar_po_kernel(
             nc.vector.scalar_tensor_tensor(result[:], primal[:, :, lo:hi], 8.0 / 9.0, diff_cols, ALU.mult, ALU.add)
             return result
 
-        def hand_on(lo, hi, result):
-            nc.scalar.copy(
+        def round_columns(copy, lo, hi, cols):
+            copy(
                 rounded[:, lo:hi, :].rearrange("p (g i) t -> p g t i", i=4),
-                result[:].rearrange("p t (g i) -> p g t i", i=4),
+                cols.rearrange("p t (g i) -> p g t i", i=4),
             )
+
+        def hand_on(lo, hi, result):
+            cut = min(hi, S - VECTOR_ROUNDS)
+            round_columns(nc.scalar.copy, lo, cut, result[:, :, 0 : cut - lo])
             nc.sync.dma_start(out_view[:, :, lo:hi], result[:])
 
         dual_steps = [(add_next, 0), (add_next, 1), (subtract_own, 0)]
@@ -212,12 +217,13 @@ def tile_picked_ytvpd_bar_po_kernel(
                 scales=out_scale[:, lo:hi],
                 in_=rounded[:, lo:hi, :].rearrange("p j t -> p (j t)"),
             )
-            if hi % HALF == 0:
-                nc.sync.dma_start(words_view[:, hi - HALF : hi], out_codes[:, hi - HALF : hi].bitcast(I32))
+            nc.sync.dma_start(words_view[:, lo:hi], out_codes[:, lo:hi].bitcast(I32))
 
-        quantise(*QUANT[0])
         for lo, hi in LAST_PIECES:
-            hand_on(lo, hi, combine(lo, hi, diffs[LAST_SPAN][:, :, lo - LAST_SPAN[0] : hi - LAST_SPAN[0]]))
+            result = combine(lo, hi, diffs[LAST_SPAN][:, :, lo - LAST_SPAN[0] : hi - LAST_SPAN[0]])
+            hand_on(lo, hi, result)
+        quantise(*QUANT[0])
+        round_columns(nc.vector.tensor_copy, S - VECTOR_ROUNDS, S, result[:, :, hi - lo - VECTOR_ROUNDS :])
         for lo, hi in QUANT[1:]:
             quantise(lo, hi)
 

from contextlib import ExitStack

import concourse.mybir as mybir

K, T, S, N = 512, 4096, 1024, 512
FLOPS = 2 * K * N * S

F32 = mybir.dt.float32
BF16 = mybir.dt.bfloat16
I32 = mybir.dt.int32
U32 = mybir.dt.uint32
U16 = mybir.dt.uint16
U8 = mybir.dt.uint8
FP8X4 = mybir.dt.float8_e4m3fn_x4
ALU = mybir.AluOpType
COPY = mybir.ActivationFunctionType.Copy
RELU = mybir.ActivationFunctionType.Relu

P = 128
PACK = 4
CHUNK = 128
CHUNKS = S // CHUNK
HALF = S // 2
PAD = 8
ZERO_SPLIT = 704
POOL_CHUNKS = 3
DUAL_STEPS_FIRST = 11
POOL_SPANS = [(0, CHUNK), (CHUNK, 3 * CHUNK), (3 * CHUNK, 5 * CHUNK)]
LAST_SPAN = (5 * CHUNK, S)
LAST_PIECES = [(640, 832), (832, 1024)]
VECTOR_ROUNDS = 96
QUANT = [(0, 512), (512, 768), (768, 1024)]


def tile_picked_ytvpd_bar_po_kernel(
    tc, x_words, x_scales, w1, dual, data, offs, out_0, out_1, out_2
):
    nc = tc.nc
    with ExitStack() as ctx:
        keep = ctx.enter_context(tc.tile_pool(name="keep", bufs=1))
        reused = ctx.enter_context(tc.tile_pool(name="reused", bufs=1))
        psum = ctx.enter_context(tc.psum_pool(name="psum", bufs=1))

        offsets = keep.tile([P, S // 16], U16, name="offsets")
        nc.sync.dma_start(offsets[:], offs)

        w_view = w1.rearrange("(p j) c -> p j c", j=PACK)
        w_raw = reused.tile([P, PACK, N], F32, name="w_raw", offset=0, align_bytes=64)
        for j in range(PACK - 1):
            nc.sync.dma_start(w_raw[:, j, :], w_view[:, j, :])

        scale_table = keep.tile([P, T], U8, name="scale_table", align_bytes=64)
        nc.vector.memset(scale_table[:].bitcast(I32)[:, 0:ZERO_SPLIT], 0)
        nc.gpsimd.memset(scale_table[:].bitcast(I32)[:, ZERO_SPLIT:], 0)
        nc.sync.dma_start(scale_table[:].bitcast(I32)[0:P:8, :], x_scales[0].bitcast(I32))
        nc.sync.dma_start(w_raw[:, PACK - 1, :], w_view[:, PACK - 1, :])

        word_table = keep.tile([P, T], I32, name="word_table", align_bytes=64)
        nc.sync.dma_start(word_table[:], x_words[0].rearrange("p c r -> p (c r)").bitcast(I32))

        picked_scales = keep.tile([P, S], U8, name="picked_scales", align_bytes=64)
        nc.vector.tensor_copy(picked_scales[:], scale_table[:].indirect(offsets[:]))
        x_scale = keep.tile([P, S], U8, name="x_scale", align_bytes=64)
        nc.vector.memset(x_scale[:].bitcast(I32), 0)
        for r in range(4):
            nc.sync.dma_start(x_scale[:].bitcast(I32)[r:P:32, :], picked_scales[:].bitcast(I32)[8 * r : P : 32, :])
        x_codes = [keep.tile([P, HALF], U32, name="x_codes%d" % h, align_bytes=64) for h in range(2)]
        for h in range(2):
            entries = offsets[:, h * HALF // 16 : (h + 1) * HALF // 16]
            nc.vector.tensor_copy(x_codes[h][:], word_table[:].bitcast(U32).indirect(entries))

        one = keep.tile([P, 1], F32, name="one")
        nc.gpsimd.memset(one[:], 1.0)
        two_c = keep.tile([P, 1], F32, name="two_c")
        nc.scalar.activation(two_c[:], one[:], RELU, scale=8.0 / 9.0)

        w_grouped = keep.tile([P, PACK, P, PACK], BF16, name="w_grouped", align_bytes=64)
        nc.scalar.copy(
            w_grouped[:].rearrange("p t m j -> p m j t"),
            w_raw[:].rearrange("p j (m t) -> p m j t", t=PACK),
        )
        w_codes = keep.tile([P, N], U32, name="w_codes", align_bytes=64)
        w_scale = keep.tile([P, N], U8, name="w_scale", align_bytes=64)
        nc.vector.quantize_mx(
            out=w_codes[:].bitcast(FP8X4),
            scales=w_scale[:],
            in_=w_grouped[:].rearrange("p t m j -> p (t m j)"),
        )

        dual_view = dual.rearrange("(p t) j -> p t j", t=PACK)
        data_view = data.rearrange("(p t) j -> p t j", t=PACK)
        out_view = out_0.rearrange("(p t) j -> p t j", t=PACK)
        lines = reused.tile([P, 2, PACK, PAD + S], F32, name="lines", offset=0, align_bytes=64)
        moved = lines[:, 0]
        primal = lines[:, 1]
        nc.gpsimd.memset(moved[:, :, 0:PAD], 0.0)

        def load_dual(lo, hi):
            nc.sync.dma_start(moved[:, :, PAD + lo : PAD + hi], dual_view[:, :, lo:hi])

        def load_data(lo, hi):
            nc.sync.dma_start(primal[:, :, lo:hi], data_view[:, :, lo:hi])

        load_dual(0, 2 * CHUNK)
        load_data(0, POOL_CHUNKS * CHUNK)
        for lo in range(2 * CHUNK, S, 2 * CHUNK):
            load_dual(lo, lo + 2 * CHUNK)
        load_data(POOL_CHUNKS * CHUNK, S)

        y = [psum.tile([P, PACK, CHUNK], F32, name="y%d" % c) for c in range(CHUNKS)]
        for c in range(CHUNKS):
            h, lo = divmod(c * CHUNK, HALF)
            for t in range(PACK):
                nc.tensor.matmul_mx(
                    out=y[c][:, t, :],
                    lhsT=w_codes[:, t * P : (t + 1) * P].bitcast(FP8X4),
                    lhsT_scale=w_scale[:, t * P : (t + 1) * P],
                    rhs=x_codes[h][:, lo : lo + CHUNK].bitcast(FP8X4),
                    rhs_scale=x_scale[:, c * CHUNK : (c + 1) * CHUNK],
                    start=True,
                    stop=True,
                )

        eighth = keep.tile([P, PACK, POOL_CHUNKS * CHUNK], F32, name="eighth")
        for c in range(POOL_CHUNKS):
            nc.scalar.activation(eighth[:, :, c * CHUNK : (c + 1) * CHUNK], y[c][:], COPY, scale=0.125)
        early = primal[:, :, 0 : POOL_CHUNKS * CHUNK]
        nc.gpsimd.tensor_tensor(early, early, eighth[:], ALU.add)

        rounded = keep.tile([P, S, PACK], BF16, name="rounded", align_bytes=64)

        def add_next(c):
            first = 1 if c == 0 else 0
            cols = moved[:, :, PAD + c * CHUNK - 1 + first : PAD + (c + 1) * CHUNK - 1]
            nc.vector.scalar_tensor_tensor(cols, y[c][:, :, first:CHUNK], 0.4, cols, ALU.mult, ALU.add)

        def subtract_own(c):
            cols = moved[:, :, PAD + c * CHUNK : PAD + (c + 1) * CHUNK]
            nc.vector.scalar_tensor_tensor(cols, y[c][:], -0.4, cols, ALU.mult, ALU.add)

        def add_eighth(c):
            cols = primal[:, :, c * CHUNK : (c + 1) * CHUNK]
            nc.vector.scalar_tensor_tensor(cols, y[c][:], 0.125, cols, ALU.mult, ALU.add)

        def clip(span):
            lo, hi = span
            width = hi - lo + 1
            raised = keep.tile([P, PACK, width], F32, name="raised%d" % lo)
            nc.scalar.activation(raised[:], moved[:, :, PAD + lo - 1 : PAD + hi], RELU, bias=one[:], scale=1.0)
            slack = keep.tile([P, PACK * width], F32, name="slack%d" % lo)
            flat = raised[:].rearrange("p t j -> p (t j)")
            nc.scalar.activation(slack[:], flat, RELU, bias=two_c[:], scale=-4.0 / 9.0)
            return slack

        def difference(engine, slack, name):
            count = slack.shape[1]
            diff = keep.tile([P, count], F32, name=name)
            engine.tensor_tensor(diff[:, 0 : count - 1], slack[:, 0 : count - 1], slack[:, 1:count], ALU.subtract)
            return diff[:].rearrange("p (t j) -> p t j", t=PACK)

        def combine(lo, hi, diff_cols):
            result = keep.tile([P, PACK, hi - lo], F32, name="result%d" % lo)
            nc.vector.scalar_tensor_tensor(result[:], primal[:, :, lo:hi], 8.0 / 9.0, diff_cols, ALU.mult, ALU.add)
            return result

        def round_columns(copy, lo, hi, cols):
            copy(
                rounded[:, lo:hi, :].rearrange("p (g i) t -> p g t i", i=4),
                cols.rearrange("p t (g i) -> p g t i", i=4),
            )

        def hand_on(lo, hi, result):
            cut = min(hi, S - VECTOR_ROUNDS)
            round_columns(nc.scalar.copy, lo, cut, result[:, :, 0 : cut - lo])
            nc.sync.dma_start(out_view[:, :, lo:hi], result[:])

        dual_steps = [(add_next, 0), (add_next, 1), (subtract_own, 0)]
        for c in range(2, CHUNKS, 2):
            dual_steps.extend([(add_next, c), (add_next, c + 1), (subtract_own, c - 1), (subtract_own, c)])
        dual_steps.append((subtract_own, CHUNKS - 1))
        slacks = {}
        diffs = {}

        def run_dual_steps(steps):
            for step, c in steps:
                step(c)
                for span in POOL_SPANS + [LAST_SPAN]:
                    if step is subtract_own and span[1] == (c + 1) * CHUNK:
                        slacks[span] = clip(span)
                        if span == POOL_SPANS[0]:
                            diffs[span] = difference(nc.gpsimd, slacks[span], "pool_diff")

        def finish_pool_span(u):
            lo, hi = POOL_SPANS[u]
            result = combine(lo, hi, diffs[lo, hi][:, :, 0 : hi - lo])
            if u + 1 < len(POOL_SPANS):
                diffs[POOL_SPANS[u + 1]] = difference(nc.gpsimd, slacks[POOL_SPANS[u + 1]], "pool_diff")
            else:
                diffs[LAST_SPAN] = difference(nc.vector, slacks[LAST_SPAN], "last_diff")
            hand_on(lo, hi, result)

        run_dual_steps(dual_steps[:DUAL_STEPS_FIRST])
        finish_pool_span(0)
        run_dual_steps(dual_steps[DUAL_STEPS_FIRST:])
        finish_pool_span(1)
        for c in range(POOL_CHUNKS, CHUNKS):
            add_eighth(c)
        finish_pool_span(2)

        out_codes = keep.tile([P, S], U32, name="out_codes", align_bytes=64)
        out_scale = keep.tile([P, S], U8, name="out_scale", align_bytes=64)
        words_view = out_1[0].rearrange("p c r -> p (c r)").bitcast(I32)

        def quantise(lo, hi):
            nc.vector.quantize_mx(
                out=out_codes[:, lo:hi].bitcast(FP8X4),
                scales=out_scale[:, lo:hi],
                in_=rounded[:, lo:hi, :].rearrange("p j t -> p (j t)"),
            )
            nc.sync.dma_start(words_view[:, lo:hi], out_codes[:, lo:hi].bitcast(I32))

        for lo, hi in LAST_PIECES:
            result = combine(lo, hi, diffs[LAST_SPAN][:, :, lo - LAST_SPAN[0] : hi - LAST_SPAN[0]])
            hand_on(lo, hi, result)
        quantise(*QUANT[0])
        round_columns(nc.vector.tensor_copy, S - VECTOR_ROUNDS, S, result[:, :, hi - lo - VECTOR_ROUNDS :])
        for lo, hi in QUANT[1:]:
            quantise(lo, hi)

        scale_rows = out_2[0].bitcast(I32).rearrange("(q r) c -> q r c", r=4)
        for q in range(4):
            queue = nc.sync if q % 2 == 0 else nc.scalar
            queue.dma_start(scale_rows[q], out_scale[:].bitcast(I32)[32 * q : 32 * q + 4, :])
